import numpy as np
import ml_dtypes


def mxq(x, axis, fmt="e4m3"):
    dtype, down = {"e4m3": (ml_dtypes.float8_e4m3fn, 7), "e5m2": (ml_dtypes.float8_e5m2, 14)}[fmt]
    v = np.moveaxis(np.asarray(x, np.float32).astype(ml_dtypes.bfloat16).astype(np.float64), axis, -1)
    blocks = v.reshape(v.shape[:-1] + (-1, 32))
    amax = np.abs(blocks).max(-1, keepdims=True)
    byte = np.maximum(np.where(amax > 0, np.frexp(amax)[1] - 1 + 127, 0) - down, 1)
    scale = np.exp2(byte - 127.0)
    codes = (blocks / scale).astype(np.float32).astype(dtype).astype(np.float64)
    return np.moveaxis((codes * scale).reshape(v.shape), -1, axis)


WIDE = False


def mx_kscale(k):
    if not WIDE:
        return np.ones(k)
    levels = np.array([10, -10, 5, -5, 0])
    if k % 512:
        return np.exp2(np.random.permutation(np.resize(levels, k // 32))).repeat(32)
    a = np.empty((k // 512, 16))
    for p in range(k // 512):
        a[p, :8] = np.random.permutation(np.resize(levels, 8))
        for g in range(8):
            far = levels[np.abs(levels - a[p, g]) >= 10]
            a[p, g + 8] = far[np.random.randint(len(far))]
    return np.exp2(a.ravel()).repeat(32)


def f64(x):
    return np.asarray(x).astype(np.float64)


def striped(idx):
    return np.tile(np.asarray(idx).reshape(-1, 16).T, (8, 1)).astype(np.uint16)


def unstriped(offs):
    return offs[:16].T.reshape(-1).astype(np.int64)


E2M1 = np.array([0.0, 0.5, 1.0, 1.5, 2.0, 3.0, 4.0, 6.0, -0.0, -0.5, -1.0, -1.5, -2.0, -3.0, -4.0, -6.0])


def pack_weight(w, fmt):
    k, n = w.shape
    w = f64(np.asarray(w, np.float32).astype(ml_dtypes.bfloat16)).reshape(k // 32, 32, n)
    amax = np.abs(w).max(1)
    if fmt == "e4m3":
        byte = np.frexp(amax)[1] - 1 + 127 - 7
    else:
        mant, ex = np.frexp(amax / 6.0)
        byte = np.where(mant > 0.5, ex, ex - 1) + 127
    byte = np.clip(np.where(amax > 0, byte, 1), 1, 254)
    scaled = (w * np.exp2(127.0 - byte)[:, None, :]).reshape(k, n).astype(np.float32)
    by_word = np.ascontiguousarray(scaled.reshape(k // 512, 128, 4, n).transpose(0, 1, 3, 2))
    if fmt == "e4m3":
        words = by_word.astype(ml_dtypes.float8_e4m3fn).view(np.uint8)
    else:
        c = by_word.astype(ml_dtypes.float4_e2m1fn).view(np.uint8) & 0xF
        words = (c[..., 0::2] | (c[..., 1::2] << 4)).reshape(k // 512, 128, 2 * n)
    return np.ascontiguousarray(words), np.ascontiguousarray(byte.astype(np.uint8).reshape(k // 512, 16, n))


def unpack_weight(words, scales, fmt):
    g, _, n = scales.shape
    words = np.ascontiguousarray(words).reshape(g, 128, n, -1)
    if fmt == "e4m3":
        vals = words.view(ml_dtypes.float8_e4m3fn).astype(np.float64)
    else:
        nib = np.empty((g, 128, n, 4), np.uint8)
        nib[..., 0::2] = words & 0xF
        nib[..., 1::2] = words >> 4
        vals = E2M1[nib]
    vals = vals * np.repeat(np.exp2(scales.astype(np.float64) - 127.0), 8, axis=1)[..., None]
    return vals.transpose(0, 1, 3, 2).reshape(g * 512, n)


D, T, I, Q, E = 512, 2048, 512, 128, 512


def setup_inputs():
    n = np.random.standard_normal
    idx = np.random.permutation(T)[:I]
    fd = mx_kscale(D)
    fi = mx_kscale(I)
    ti = np.ones(T)
    ti[idx] = fi
    keysp = pack_weight(n((D, T)) / fd[:, None], "e4m3")
    return {
        "query": (n((D, Q)) * 1.0 / np.sqrt(D) * fd[:, None]).astype(np.float32),
        "keys_words": keysp[0],
        "keys_scales": keysp[1],
        "lowend": np.tile(np.random.uniform(-1.5, 0.0, T), (128, 1)).astype(np.float32),
        "highend": np.tile(np.random.uniform(0.0, 1.5, T), (128, 1)).astype(np.float32),
        "lam": (np.random.uniform(0.8, 2.0, (Q, 1))).astype(np.float32),
        "mem": (np.random.uniform(0.3, 0.7, (1, Q))).astype(np.float32),
        "os": (np.random.uniform(4.0, 16.0, (1, I)) * fi).astype(np.float32),
        "vals": (n((E, T)) / ti).astype(np.float32),
        "vsharp": (np.random.uniform(0.6, 1.2, (Q, 1))).astype(np.float32),
        "offs": striped(idx),
    }


def reference(query, keys_words, keys_scales, lowend, highend, lam, mem, os, vals, vsharp, offs):
    idx = unstriped(offs)
    keysu = unpack_weight(keys_words, keys_scales, "e4m3")
    queryq = mxq(f64(query), 0, "e4m3")
    keysidxg = keysu[:, idx]
    a = queryq.T @ keysidxg
    s = np.minimum(a - f64(lowend)[:1][:, idx], f64(highend)[:1][:, idx] - a) * f64(lam)
    p = np.exp(s - np.max(s, axis=1, keepdims=True))
    r = p / np.sum(p, axis=1, keepdims=True)
    rt = r.T
    rt1 = np.pad(rt, ((0, 0), (1, 0)))[:, :Q]
    w0 = rt - (rt - rt1) * f64(mem)
    w = w0.T
    wo1 = w * f64(os)
    wt1 = wo1.T
    vt1 = f64(vals)[:, idx].T
    wt1q = mxq(wt1, 0, "e4m3")
    vt1q = mxq(vt1, 0, "e4m3")
    o = wt1q.T @ vt1q
    oz = o * f64(vsharp)
    oe = np.exp(oz - np.max(oz, axis=1, keepdims=True))
    y = oe / np.sum(oe, axis=1, keepdims=True) * 512.0
    return y

from contextlib import ExitStack

import concourse.mybir as mybir
from concourse.masks import make_identity

D, T, I, Q, E = 512, 2048, 512, 128, 512
FLOPS = 2 * D * Q * I + 2 * I * Q * E
BYTES = 4 * D * Q + D * T + D * T // 32 + 2 * 4 * T + 3 * 4 * Q + 4 * I + 4 * E * T + 2 * 128 * (I // 16) + 4 * Q * E

F32 = mybir.dt.float32
BF16 = mybir.dt.bfloat16
I32 = mybir.dt.int32
U32 = mybir.dt.uint32
U16 = mybir.dt.uint16
U8 = mybir.dt.uint8
FP8X4 = mybir.dt.float8_e4m3fn_x4
ALU = mybir.AluOpType
ACT = mybir.ActivationFunctionType

P = 128
PACK = 4
LAST = P - 1


def tile_attend_interval_overrows_readshares_kernel(
    tc, query, keys_words, keys_scales, lowend, highend, lam, mem, slot_factor, vals, vsharp, offs, out
):
    nc = tc.nc
    with ExitStack() as ctx:
        sb = ctx.enter_context(tc.tile_pool(name="sb", bufs=1))
        ps = ctx.enter_context(tc.psum_pool(name="ps", bufs=1))

        offsets = sb.tile([P, I // 16], U16, name="offsets")
        q_raw = sb.tile([P, PACK, Q], F32, name="q_raw")
        key_pool = sb.tile([P, T], I32, name="key_pool")
        scale_pool = sb.tile([P, T], U8, name="scale_pool")
        low_pool = sb.tile([P, T], F32, name="low_pool")
        high_pool = sb.tile([P, T], F32, name="high_pool")
        val_pool = [sb.tile([P, T], F32, name="val_pool%d" % b) for b in range(E // P)]
        mem_row = sb.tile([P, Q + 8], F32, name="mem_row")
        lam_col = sb.tile([P, 1], F32, name="lam_col")
        sharp_col = sb.tile([P, 1], F32, name="sharp_col")
        factor = sb.tile([P, PACK], F32, name="factor")
        ident = sb.tile([P, P], F32, name="ident")

        nc.vector.memset(scale_pool[:].bitcast(I32), 0)
        nc.vector.memset(mem_row[:], 0.0)
        nc.vector.memset(low_pool[0:LAST, :], 0.0)
        nc.vector.memset(high_pool[0:LAST, :], 0.0)
        nc.gpsimd.dma_start(out=lam_col[:], in_=lam)
        make_identity(nc, ident[:])

        nc.sync.dma_start(offsets[:], offs)
        nc.sync.dma_start(out=key_pool[:], in_=keys_words[0].rearrange("p n t -> p (n t)").bitcast(I32))
        nc.scalar.dma_start(out=low_pool[LAST:P, :], in_=lowend[0:1, :])
        nc.scalar.dma_start(out=high_pool[LAST:P, :], in_=highend[0:1, :])
        for quad in range(4):
            nc.scalar.dma_start(
                out=scale_pool[32 * quad : 32 * quad + 4, :].bitcast(I32),
                in_=keys_scales[0][4 * quad : 4 * quad + 4, :].bitcast(I32),
            )
        nc.sync.dma_start(out=q_raw[:], in_=query.rearrange("(p j) q -> p j q", j=PACK))
        nc.sync.dma_start(out=val_pool[0][:], in_=vals[0:P, :])
        nc.sync.dma_start(out=mem_row[0:1, 0:Q], in_=mem)
        nc.sync.dma_start(out=factor[:], in_=slot_factor.rearrange("o (p t) -> (o p) t", t=PACK))
        nc.sync.dma_start(out=sharp_col[:], in_=vsharp)
        for b in range(1, E // P):
            nc.sync.dma_start(out=val_pool[b][:], in_=vals[b * P : (b + 1) * P, :])

        ends = []
        for name, pool_tile, tag in (("low", low_pool, "turn0"), ("high", high_pool, "turn1")):
            row = sb.tile([P, I], F32, name=name + "_row")
            nc.scalar.activation(row[:], pool_tile[:].indirect(offsets[:]), ACT.Copy)
            turned = ps.tile([P, PACK, P], F32, name=name + "_turned", tag=tag)
            for c in range(PACK):
                nc.tensor.transpose(turned[:, c, :], row[:, c * P : (c + 1) * P], ident[:])
            cols = sb.tile([P, PACK], F32, name=name + "_cols")
            nc.scalar.copy(out=cols[:], in_=turned[:, :, LAST])
            ends.append(cols)
        low_cols, high_cols = ends

        k_scales = sb.tile([P, I], U8, name="k_scales", align_bytes=64)
        k_codes = sb.tile([P, I], U32, name="k_codes", align_bytes=64)
        nc.vector.tensor_copy(out=k_scales[:], in_=scale_pool[:].indirect(offsets[:]))
        outside = sb.tile([P, PACK, Q], F32, name="outside")
        below = sb.tile([P, PACK, Q], F32, name="below")
        z_turned = ps.tile([P, I], F32, name="z_turned", tag="zt")
        for h in range(2):
            nc.vector.tensor_copy(
                out=k_codes[:, 256 * h : 256 * (h + 1)],
                in_=key_pool[:].bitcast(U32).indirect(offsets[:, 16 * h : 16 * (h + 1)]),
            )
        q_bf = sb.tile([P, Q, PACK], BF16, name="q_bf", align_bytes=64)
        q_codes = sb.tile([P, Q], U32, name="q_codes", align_bytes=64)
        q_scales = sb.tile([P, Q], U8, name="q_scales", align_bytes=64)
        nc.vector.tensor_copy(out=q_bf[:], in_=q_raw[:].rearrange("p j q -> p q j"))
        nc.vector.quantize_mx(
            out=q_codes[:].bitcast(FP8X4), scales=q_scales[:], in_=q_bf[:].rearrange("p q j -> p (q j)")
        )

        for h in range(2):
            score = ps.tile([P, 2, Q], F32, name="score%d" % h, tag="score%d" % h)
            for j in range(2):
                c = 2 * h + j
                nc.tensor.matmul_mx(
                    out=score[:, j, :],
                    lhsT=k_codes[:, c * P : (c + 1) * P].bitcast(FP8X4),
                    lhsT_scale=k_scales[:, c * P : (c + 1) * P],
                    rhs=q_codes[:].bitcast(FP8X4),
                    rhs_scale=q_scales[:],
                    start=True,
                    stop=True,
                )
            for j in range(2):
                c = 2 * h + j
                nc.scalar.activation(
                    below[:, c, :], score[:, j, :], ACT.Identity, bias=low_cols[:, c : c + 1], scale=-1.0
                )
            for j in range(2):
                c = 2 * h + j
                nc.vector.scalar_tensor_tensor(
                    outside[:, c, :], score[:, j, :], high_cols[:, c : c + 1], below[:, c, :], ALU.subtract, ALU.max
                )
            for j in range(2):
                c = 2 * h + j
                nc.tensor.transpose(z_turned[:, c * P : (c + 1) * P], outside[:, c, :], ident[:])

        mem_turned = ps.tile([P, 2, P], F32, name="mem_turned", tag="memt")
        nc.tensor.transpose(mem_turned[:, 0, :], mem_row[:, 0:P], ident[:])
        nc.tensor.transpose(mem_turned[:, 1, :], mem_row[:, 1 : P + 1], ident[:])
        keep = sb.tile([P, 1], F32, name="keep")
        carry = sb.tile([P, 1], F32, name="carry")
        nc.vector.tensor_scalar(keep[:], mem_turned[:, 0, 0:1], -1.0, 1.0, ALU.mult, ALU.add)
        nc.vector.tensor_copy(out=carry[:], in_=mem_turned[:, 1, 0:1])
        neg_sharp = sb.tile([P, 1], F32, name="neg_sharp")
        nc.vector.tensor_scalar(neg_sharp[:], sharp_col[:], -1.0, None, ALU.mult)

        neg_score = sb.tile([P, PACK, P], F32, name="neg_score")
        neg_top = sb.tile([P, 1], F32, name="neg_top")
        nc.vector.tensor_scalar(
            neg_score[:], z_turned[:].rearrange("p (s t) -> p t s", t=PACK), lam_col[:], None, ALU.mult, ALU.min,
            accum_out=neg_top[:],
        )
        p_tile = sb.tile([P, I], F32, name="p_tile")
        p_sum = sb.tile([P, 1], F32, name="p_sum")
        nc.scalar.activation(
            p_tile[:], neg_score[:].rearrange("p t s -> p (t s)"), ACT.Exp, bias=neg_top[:], scale=-1.0,
            accum_out=p_sum[:],
        )
        p_inv = sb.tile([P, 1], F32, name="p_inv")
        nc.vector.reciprocal(p_inv[:], p_sum[:])

        own = sb.tile([P, I], F32, name="own")
        handed = sb.tile([P, I], F32, name="handed")
        w_bf = sb.tile([P, Q, PACK], BF16, name="w_bf", align_bytes=64)
        for h in range(2):
            cols = slice(256 * h, 256 * (h + 1))
            nc.vector.tensor_scalar(own[:, cols], p_tile[:, cols], p_inv[:], keep[:], ALU.mult, ALU.mult)
            nc.vector.tensor_scalar(handed[:, cols], p_tile[:, cols], p_inv[:], carry[:], ALU.mult, ALU.mult)
        for h in range(2):
            mix = ps.tile([P, 3 * P], F32, name="mix%d" % h, tag="mix%d" % h)
            nc.tensor.matmul(mix[:, 2 * P : 3 * P], lhsT=ident[:], rhs=ident[:], is_transpose=True, start=True, stop=False)
            for j in range(2):
                t = 2 * h + j
                nc.tensor.matmul(
                    mix[:, j * P : (j + 1) * P], lhsT=own[:, t * P : (t + 1) * P], rhs=ident[:],
                    is_transpose=True, start=False, stop=False,
                )
            for j in range(2):
                t = 2 * h + j
                nc.tensor.matmul(
                    mix[:, j * P + 1 : (j + 1) * P + 1], lhsT=handed[:, t * P : (t + 1) * P], rhs=ident[:],
                    is_transpose=True, start=False, stop=(j == 1),
                )
            nc.vector.tensor_tensor(
                w_bf[:, :, 2 * h : 2 * h + 2],
                mix[:, 0 : 2 * P].rearrange("p (j q) -> p q j", j=2),
                factor[:, 2 * h : 2 * h + 2].unsqueeze(1).to_broadcast([P, Q, 2]),
                ALU.mult,
            )
        w_codes = sb.tile([P, Q], U32, name="w_codes", align_bytes=64)
        w_scales = sb.tile([P, Q], U8, name="w_scales", align_bytes=64)
        nc.vector.quantize_mx(
            out=w_codes[:].bitcast(FP8X4), scales=w_scales[:], in_=w_bf[:].rearrange("p q t -> p (q t)")
        )

        last = E // P - 1
        read_early = ps.tile([P, last * P], F32, name="read_early", tag="score0")
        read_last = ps.tile([P, P], F32, name="read_last", tag="score1")
        for b in range(E // P):
            picked = sb.tile([P, I], BF16, name="picked%d" % b)
            if b < last:
                nc.scalar.activation(picked[:], val_pool[b][:].indirect(offsets[:]), ACT.Copy)
            else:
                nc.scalar.activation(picked[:, 0:256], val_pool[b][:].indirect(offsets[:, 0:16]), ACT.Copy)
                nc.vector.tensor_copy(out=picked[:, 256:512], in_=val_pool[b][:].indirect(offsets[:, 16:32]))
            words = picked[:].bitcast(F32)
            v_turned = ps.tile([P, 2, P], F32, name="v_turned%d" % b, tag="turn%d" % (b % 2))
            for u in range(2):
                nc.tensor.transpose(v_turned[:, u, :], words[:, u : 2 * P : 2], ident[:])
            v_bf = sb.tile([P, P * PACK], BF16, name="v_bf%d" % b, align_bytes=64)
            nc.vector.tensor_copy(
                out=v_bf[:].bitcast(F32).rearrange("p (e u) -> p e u", u=2),
                in_=v_turned[:].rearrange("p u e -> p e u"),
            )
            v_codes = sb.tile([P, P], U32, name="v_codes%d" % b, align_bytes=64)
            v_scales = sb.tile([P, P], U8, name="v_scales%d" % b, align_bytes=64)
            nc.vector.quantize_mx(out=v_codes[:].bitcast(FP8X4), scales=v_scales[:], in_=v_bf[:])
            target = read_early[:, b * P : (b + 1) * P] if b < last else read_last[:]
            nc.tensor.matmul_mx(
                out=target,
                lhsT=w_codes[:].bitcast(FP8X4),
                lhsT_scale=w_scales[:],
                rhs=v_codes[:].bitcast(FP8X4),
                rhs_scale=v_scales[:],
                start=True,
                stop=True,
            )

        neg_oz = sb.tile([P, E], F32, name="neg_oz")
        neg_top_early = sb.tile([P, 1], F32, name="neg_top_early")
        neg_top_all = sb.tile([P, 1], F32, name="neg_top_all")
        nc.vector.tensor_scalar(
            neg_oz[:, 0 : last * P], read_early[:], neg_sharp[:], None, ALU.mult, ALU.min, accum_out=neg_top_early[:]
        )
        nc.vector.tensor_scalar(
            neg_oz[:, last * P : E], read_last[:], neg_sharp[:], neg_top_early[:], ALU.mult, ALU.min,
            accum_out=neg_top_all[:],
        )
        oe = sb.tile([P, E], F32, name="oe")
        oe_sum = sb.tile([P, 1], F32, name="oe_sum")
        nc.scalar.activation(oe[:], neg_oz[:], ACT.Exp, bias=neg_top_all[:], scale=-1.0, accum_out=oe_sum[:])
        oe_inv = sb.tile([P, 1], F32, name="oe_inv")
        nc.vector.reciprocal(oe_inv[:], oe_sum[:])
        result = sb.tile([P, E], F32, name="result")
        nc.vector.tensor_scalar(result[:], oe[:], oe_inv[:], float(E), ALU.mult, ALU.mult)
        nc.sync.dma_start(out=out, in_=result[:])
